import numpy as np
import ml_dtypes


def mxq(x, axis, fmt="e4m3"):
    dtype, down = {"e4m3": (ml_dtypes.float8_e4m3fn, 7), "e5m2": (ml_dtypes.float8_e5m2, 14)}[fmt]
    v = np.moveaxis(np.asarray(x, np.float32).astype(ml_dtypes.bfloat16).astype(np.float64), axis, -1)
    blocks = v.reshape(v.shape[:-1] + (-1, 32))
    amax = np.abs(blocks).max(-1, keepdims=True)
    byte = np.maximum(np.where(amax > 0, np.frexp(amax)[1] - 1 + 127, 0) - down, 1)
    scale = np.exp2(byte - 127.0)
    codes = (blocks / scale).astype(np.float32).astype(dtype).astype(np.float64)
    return np.moveaxis((codes * scale).reshape(v.shape), -1, axis)


WIDE = False


def mx_kscale(k):
    if not WIDE:
        return np.ones(k)
    levels = np.array([10, -10, 5, -5, 0])
    if k % 512:
        return np.exp2(np.random.permutation(np.resize(levels, k // 32))).repeat(32)
    a = np.empty((k // 512, 16))
    for p in range(k // 512):
        a[p, :8] = np.random.permutation(np.resize(levels, 8))
        for g in range(8):
            far = levels[np.abs(levels - a[p, g]) >= 10]
            a[p, g + 8] = far[np.random.randint(len(far))]
    return np.exp2(a.ravel()).repeat(32)


def f64(x):
    return np.asarray(x).astype(np.float64)


def striped(idx):
    return np.tile(idx.reshape(-1, 16).T, (8, 1)).astype(np.uint16)


def unstriped(offs):
    return offs[:16].T.reshape(-1).astype(np.int64)


def pack_weight(w):
    k, n = w.shape
    w = f64(np.asarray(w, np.float32).astype(ml_dtypes.bfloat16)).reshape(k // 32, 32, n)
    amax = np.abs(w).max(1)
    byte = np.clip(np.where(amax > 0, np.frexp(amax)[1] - 1 + 127 - 7, 1), 1, 254)
    scaled = (w * np.exp2(127.0 - byte)[:, None, :]).reshape(k, n).astype(np.float32)
    words = np.ascontiguousarray(scaled.reshape(k // 512, 128, 4, n).transpose(0, 1, 3, 2)).astype(ml_dtypes.float8_e4m3fn).view(np.uint8)
    return words, np.ascontiguousarray(byte.astype(np.uint8).reshape(k // 512, 16, n))


def unpack_weight(words, scales):
    g, p, n, _ = words.shape
    vals = np.ascontiguousarray(words).view(ml_dtypes.float8_e4m3fn).astype(np.float64) * np.repeat(np.exp2(scales.astype(np.float64) - 127.0), 8, axis=1)[..., None]
    return vals.transpose(0, 1, 3, 2).reshape(g * 512, n)


def gelu(v):
    return 0.5 * v * (1.0 + np.tanh(np.sqrt(2.0 / np.pi) * (v + 0.044715 * v**3)))


K, T, S, V, H, N, J = 1024, 2048, 1024, 512, 512, 128, 512


def setup_inputs():
    n = np.random.standard_normal
    s = mx_kscale(K)[:, None]
    u = mx_kscale(H)
    r = mx_kscale(J)[:, None]
    packed_xT = pack_weight(n((K, T)) * s)
    packed_w4 = pack_weight(n((H, N)) / np.sqrt(H) / u[:, None])
    return {
        "x_words": packed_xT[0],
        "x_scales": packed_xT[1],
        "eT": (n((J, V)) * r).astype(np.float32),
        "w1": (n((K, H)) / np.sqrt(3 * K) / s * u).astype(np.float32),
        "w2": (n((K, H)) / np.sqrt(3 * K) / s * u).astype(np.float32),
        "w3": (n((J, H)) / np.sqrt(3 * J) / r * u).astype(np.float32),
        "w4_words": packed_w4[0],
        "w4_scales": packed_w4[1],
        "offs": striped(np.random.permutation(T)[:S]),
    }


def reference(x_words, x_scales, eT, w1, w2, w3, w4_words, w4_scales, offs):
    xq = unpack_weight(x_words, x_scales)[:, unstriped(offs)]
    h = gelu(mxq(f64(w1), 0, "e4m3").T @ xq[:, :V] + mxq(f64(w2), 0, "e4m3").T @ xq[:, V:2 * V] + mxq(f64(w3), 0, "e4m3").T @ mxq(f64(eT), 0, "e4m3"))
    return unpack_weight(w4_words, w4_scales).T @ mxq(h, 0, "e4m3")

@@ -1,0 +1,198 @@
+from contextlib import ExitStack
+
+import concourse.mybir as mybir
+from concourse.masks import make_identity
+
+K, T, S, V, H, N, J = 1024, 2048, 1024, 512, 512, 128, 512
+FLOPS = 2 * V * H * (2 * K + J) + 2 * V * H * N
+
+F32 = mybir.dt.float32
+BF16 = mybir.dt.bfloat16
+I32 = mybir.dt.int32
+U32 = mybir.dt.uint32
+U16 = mybir.dt.uint16
+U8 = mybir.dt.uint8
+FP8X4 = mybir.dt.float8_e4m3fn_x4
+GELU = mybir.ActivationFunctionType.Gelu_apprx_tanh
+
+P = 128
+PACK = 4
+K_PASS = P * PACK
+PASSES = K // K_PASS
+EDGE_TILE = 128
+EDGE_TILES = V // EDGE_TILE
+LIST_COL = 16
+
+
+def tile_picked_edgeup_gelu_p_kernel(
+    tc, x_words, x_scales, eT, w1, w2, w3, w4_words, w4_scales, offs, out
+):
+    nc = tc.nc
+    with ExitStack() as ctx:
+        keep = ctx.enter_context(tc.tile_pool(name="keep", bufs=1))
+        psum = ctx.enter_context(tc.psum_pool(name="psum", bufs=1))
+
+        def load_rows(name, rows):
+            raw = keep.tile([P, PACK, rows.shape[1]], F32, name=name + "_raw")
+            nc.sync.dma_start(out=raw[:], in_=rows.rearrange("(p j) c -> p j c", j=PACK))
+            return raw
+
+        def interleave(name, raw, cols, on_scalar):
+            width = cols.stop - cols.start
+            grouped = keep.tile([P, width * PACK], BF16, name=name + "_grouped", align_bytes=64)
+            dst = grouped[:].rearrange("p (c i j) -> p c j i", i=4, j=PACK)
+            src = raw[:, :, cols].rearrange("p j (c i) -> p c j i", i=4)
+            if on_scalar:
+                nc.scalar.copy(out=dst, in_=src)
+            else:
+                nc.vector.tensor_copy(out=dst, in_=src)
+            return grouped
+
+        def mx_tiles(name, width):
+            codes = keep.tile([P, width], U32, name=name + "_codes", align_bytes=64)
+            scales = keep.tile([P, width], U8, name=name + "_scales", align_bytes=64)
+            return codes, scales
+
+        def quantize(mx, cols, grouped):
+            nc.vector.quantize_mx(out=mx[0][:, cols].bitcast(FP8X4), scales=mx[1][:, cols], in_=grouped[:])
+
+        def load_words(name, words):
+            tile = keep.tile([P, words.shape[1]], U32, name=name, align_bytes=64)
+            return tile, words.rearrange("p n t -> p (n t)").bitcast(I32)
+
+        offsets = keep.tile([P, S // LIST_COL], U16, name="offsets")
+        x_plane = keep.tile([P, T], U8, name="x_plane", align_bytes=64)
+        w4_plane = keep.tile([P, N], U8, name="w4_plane", align_bytes=64)
+        nc.vector.memset(x_plane[:].bitcast(I32), 0)
+        nc.vector.memset(w4_plane[:].bitcast(I32), 0)
+
+        raw_w = {}
+        x_table = []
+        raw_w[0, 0] = load_rows("w1_0", w1[0:K_PASS, :])
+        nc.sync.dma_start(offsets[:], offs)
+        for q in range(4):
+            nc.scalar.dma_start(
+                out=x_plane[32 * q : 32 * q + 4 * PASSES, :].bitcast(I32),
+                in_=x_scales[:, 4 * q : 4 * q + 4, :].bitcast(I32),
+            )
+        tile0, src0 = load_words("x_table0", x_words[0])
+        nc.sync.dma_start(out=tile0[:].bitcast(I32), in_=src0)
+        x_table.append(tile0)
+        raw_w[1, 0] = load_rows("w2_0", w2[0:K_PASS, :])
+        tile1, src1 = load_words("x_table1", x_words[1])
+        nc.sync.dma_start(out=tile1[:].bitcast(I32), in_=src1)
+        x_table.append(tile1)
+        raw_w[0, 1] = load_rows("w1_1", w1[K_PASS:K, :])
+        w4_codes, w4_src = load_words("w4_codes", w4_words[0])
+        nc.sync.dma_start(out=w4_codes[:].bitcast(I32), in_=w4_src)
+        for q in range(4):
+            nc.sync.dma_start(
+                out=w4_plane[32 * q : 32 * q + 4, :].bitcast(I32),
+                in_=w4_scales[0, 4 * q : 4 * q + 4, :].bitcast(I32),
+            )
+        raw_w[1, 1] = load_rows("w2_1", w2[K_PASS:K, :])
+        half = V // 2
+        raw_e0 = load_rows("e_0", eT[:, 0:half])
+        raw_w3 = [load_rows("w3_%d" % a, w3[:, a * half : (a + 1) * half]) for a in range(2)]
+        raw_e1 = load_rows("e_1", eT[:, half:V])
+
+        identity = keep.tile([P, P], F32, name="identity")
+        make_identity(nc, identity[:])
+
+        h_bank = [psum.tile([P, H], F32, name="h_bank%d" % c) for c in range(EDGE_TILES)]
+        t_bank = [psum.tile([P, 2, EDGE_TILE], F32, name="t_bank%d" % c) for c in range(EDGE_TILES)]
+
+        picked_plane = keep.tile([P, S], U8, name="picked_plane", align_bytes=64)
+        nc.vector.tensor_copy(picked_plane[:], x_plane[:].indirect(offsets[:]))
+
+        def gather_words(side, z):
+            picked = keep.tile([P, V], U32, name="picked%d_%d" % (side, z), align_bytes=64)
+            cols = slice(side * V // LIST_COL, (side + 1) * V // LIST_COL)
+            nc.vector.tensor_copy(picked[:], x_table[z][:].indirect(offsets[:, cols]))
+            return picked
+
+        def node_pass(side, z, picked, w_mx):
+            for c in range(EDGE_TILES):
+                e0 = c * EDGE_TILE
+                nc.tensor.matmul_mx(
+                    out=h_bank[c][:],
+                    lhsT=picked[:, e0 : e0 + EDGE_TILE].bitcast(FP8X4),
+                    lhsT_scale=picked_plane[4 * z : P, side * V + e0 : side * V + e0 + EDGE_TILE],
+                    rhs=w_mx[0][:].bitcast(FP8X4),
+                    rhs_scale=w_mx[1][:],
+                    start=(side == 0 and z == 0),
+                    stop=False,
+                )
+
+        whole = slice(0, H)
+        lo, hi = slice(0, half), slice(half, H)
+        for z in range(PASSES):
+            picked = [gather_words(side, z) for side in range(2)]
+            for side in range(2):
+                name = "w%d_%d" % (side + 1, z)
+                w_mx = mx_tiles(name, H)
+                if side == 1 and z == PASSES - 1:
+                    g_lo = interleave(name + "lo", raw_w[side, z], lo, True)
+                    g_hi = interleave(name + "hi", raw_w[side, z], hi, False)
+                    quantize(w_mx, hi, g_hi)
+                    quantize(w_mx, lo, g_lo)
+                else:
+                    quantize(w_mx, whole, interleave(name, raw_w[side, z], whole, True))
+                node_pass(side, z, picked[side], w_mx)
+
+        e_mx = [mx_tiles("e%d" % c, EDGE_TILE) for c in range(EDGE_TILES)]
+        tile_cols = slice(0, EDGE_TILE)
+
+        def edge_pair(raw, first):
+            grouped = [
+                interleave("e%d" % (first + a), raw, slice(a * EDGE_TILE, (a + 1) * EDGE_TILE), False) for a in range(2)
+            ]
+            for a in range(2):
+                quantize(e_mx[first + a], tile_cols, grouped[a])
+
+        edge_pair(raw_e0, 0)
+        w3_mx = mx_tiles("w3", H)
+        for a in range(2):
+            quantize(w3_mx, (lo, hi)[a], interleave("w3_%d" % a, raw_w3[a], lo, False))
+        edge_pair(raw_e1, 2)
+
+        for c in range(EDGE_TILES):
+            nc.tensor.matmul_mx(
+                out=h_bank[c][:],
+                lhsT=e_mx[c][0][:].bitcast(FP8X4),
+                lhsT_scale=e_mx[c][1][:],
+                rhs=w3_mx[0][:].bitcast(FP8X4),
+                rhs_scale=w3_mx[1][:],
+                start=False,
+                stop=True,
+            )
+
+        for c in range(EDGE_TILES):
+            h_rows = keep.tile([P, H], BF16, name="h_rows%d" % c, align_bytes=64)
+            nc.scalar.activation(
+                out=h_rows[:].rearrange("v (u p e) -> v u p e", u=2, e=2),
+                in_=h_bank[c][:].rearrange("v (p u e) -> v u p e", u=2, e=2),
+                func=GELU,
+            )
+            pairs = h_rows[:].bitcast(F32)
+            for u in range(2):
+                nc.tensor.transpose(t_bank[c][:, u, :], pairs[:, u * P : (u + 1) * P], identity[:])
+            h_grouped = keep.tile([P, EDGE_TILE * PACK], BF16, name="h_grouped%d" % c, align_bytes=64)
+            nc.vector.tensor_copy(
+                out=h_grouped[:].bitcast(F32).rearrange("p (v u) -> p v u", u=2),
+                in_=t_bank[c][:].rearrange("p u v -> p v u"),
+            )
+            h_mx = mx_tiles("h%d" % c, EDGE_TILE)
+            quantize(h_mx, tile_cols, h_grouped)
+            nc.tensor.matmul_mx(
+                out=h_bank[c][:, tile_cols],
+                lhsT=w4_codes[:].bitcast(FP8X4),
+                lhsT_scale=w4_plane[:],
+                rhs=h_mx[0][:].bitcast(FP8X4),
+                rhs_scale=h_mx[1][:],
+                start=True,
+                stop=True,
+            )
+            result = keep.tile([P, EDGE_TILE], F32, name="result%d" % c)
+            nc.scalar.copy(out=result[:], in_=h_bank[c][:, tile_cols])
+            nc.sync.dma_start(out=out[:, c * EDGE_TILE : (c + 1) * EDGE_TILE], in_=result[:])

@@ -22,6 +22,7 @@ PASSES = K // K_PASS
 EDGE_TILE = 128
 EDGE_TILES = V // EDGE_TILE
 LIST_COL = 16
+E_LOADS = (1, 2, 1)
 
 
 def tile_picked_edgeup_gelu_p_kernel(
@@ -56,45 +57,55 @@ def tile_picked_edgeup_gelu_p_kernel(
         def quantize(mx, cols, grouped):
             nc.vector.quantize_mx(out=mx[0][:, cols].bitcast(FP8X4), scales=mx[1][:, cols], in_=grouped[:])
 
-        def load_words(name, words):
+        def load_words(name, words, queue):
             tile = keep.tile([P, words.shape[1]], U32, name=name, align_bytes=64)
-            return tile, words.rearrange("p n t -> p (n t)").bitcast(I32)
+            queue.dma_start(out=tile[:].bitcast(I32), in_=words.rearrange("p n t -> p (n t)").bitcast(I32))
+            return tile
 
         offsets = keep.tile([P, S // LIST_COL], U16, name="offsets")
         x_plane = keep.tile([P, T], U8, name="x_plane", align_bytes=64)
         w4_plane = keep.tile([P, N], U8, name="w4_plane", align_bytes=64)
         nc.vector.memset(x_plane[:].bitcast(I32), 0)
         nc.vector.memset(w4_plane[:].bitcast(I32), 0)
+        warm = keep.tile([P, 2], F32, name="warm")
+        nc.vector.memset(warm[:, 0:1], 0.0)
+        nc.scalar.activation(out=warm[:, 1:2], in_=warm[:, 0:1], func=GELU)
 
-        raw_w = {}
-        x_table = []
-        raw_w[0, 0] = load_rows("w1_0", w1[0:K_PASS, :])
-        nc.sync.dma_start(offsets[:], offs)
-        for q in range(4):
-            nc.scalar.dma_start(
-                out=x_plane[32 * q : 32 * q + 4 * PASSES, :].bitcast(I32),
-                in_=x_scales[:, 4 * q : 4 * q + 4, :].bitcast(I32),
-            )
-        tile0, src0 = load_words("x_table0", x_words[0])
-        nc.sync.dma_start(out=tile0[:].bitcast(I32), in_=src0)
-        x_table.append(tile0)
-        raw_w[1, 0] = load_rows("w2_0", w2[0:K_PASS, :])
-        tile1, src1 = load_words("x_table1", x_words[1])
-        nc.sync.dma_start(out=tile1[:].bitcast(I32), in_=src1)
-        x_table.append(tile1)
-        raw_w[0, 1] = load_rows("w1_1", w1[K_PASS:K, :])
-        w4_codes, w4_src = load_words("w4_codes", w4_words[0])
-        nc.sync.dma_start(out=w4_codes[:].bitcast(I32), in_=w4_src)
-        for q in range(4):
-            nc.sync.dma_start(
-                out=w4_plane[32 * q : 32 * q + 4, :].bitcast(I32),
-                in_=w4_scales[0, 4 * q : 4 * q + 4, :].bitcast(I32),
-            )
-        raw_w[1, 1] = load_rows("w2_1", w2[K_PASS:K, :])
+        def load_x_scales():
+            for q in range(4):
+                nc.sync.dma_start(
+                    out=x_plane[32 * q : 32 * q + 4 * PASSES, :].bitcast(I32),
+                    in_=x_scales[:, 4 * q : 4 * q + 4, :].bitcast(I32),
+                )
+
+        def load_w4():
+            codes = load_words("w4_codes", w4_words[0], nc.sync)
+            for q in range(4):
+                nc.sync.dma_start(
+                    out=w4_plane[32 * q : 32 * q + 4, :].bitcast(I32),
+                    in_=w4_scales[0, 4 * q : 4 * q + 4, :].bitcast(I32),
+                )
+            return codes
+
         half = V // 2
-        raw_e0 = load_rows("e_0", eT[:, 0:half])
+        raw_w = {}
+        x_table = {}
+        x_table[0] = load_words("x_table0", x_words[0], nc.sync)
+        load_x_scales()
+        nc.sync.dma_start(offsets[:], offs)
+        raw_w[0, 0] = load_rows("w1_0", w1[0:K_PASS, :])
+        x_table[1] = load_words("x_table1", x_words[1], nc.sync)
+        raw_w[1, 0] = load_rows("w2_0", w2[0:K_PASS, :])
+        w4_codes = load_w4()
+        raw_w[0, 1] = load_rows("w1_1", w1[K_PASS:K, :])
+        raw_w[1, 1] = load_rows("w2_1", w2[K_PASS:K, :])
         raw_w3 = [load_rows("w3_%d" % a, w3[:, a * half : (a + 1) * half]) for a in range(2)]
-        raw_e1 = load_rows("e_1", eT[:, half:V])
+        raw_e = []
+        first = 0
+        for tiles in E_LOADS:
+            raw = load_rows("e_%d" % first, eT[:, first * EDGE_TILE : (first + tiles) * EDGE_TILE])
+            raw_e.extend([(raw, slice(a * EDGE_TILE, (a + 1) * EDGE_TILE)) for a in range(tiles)])
+            first = first + tiles
 
         identity = keep.tile([P, P], F32, name="identity")
         make_identity(nc, identity[:])
@@ -103,7 +114,9 @@ def tile_picked_edgeup_gelu_p_kernel(
         t_bank = [psum.tile([P, 2, EDGE_TILE], F32, name="t_bank%d" % c) for c in range(EDGE_TILES)]
 
         picked_plane = keep.tile([P, S], U8, name="picked_plane", align_bytes=64)
-        nc.vector.tensor_copy(picked_plane[:], x_plane[:].indirect(offsets[:]))
+
+        def gather_plane():
+            nc.vector.tensor_copy(picked_plane[:], x_plane[:].indirect(offsets[:]))
 
         def gather_words(side, z):
             picked = keep.tile([P, V], U32, name="picked%d_%d" % (side, z), align_bytes=64)
@@ -126,35 +139,33 @@ def tile_picked_edgeup_gelu_p_kernel(
 
         whole = slice(0, H)
         lo, hi = slice(0, half), slice(half, H)
+        gather_plane()
+        picked = {(side, z): gather_words(side, z) for z in range(PASSES) for side in range(2)}
+        plan = {(0, 0): "scalar", (1, 0): "scalar", (0, 1): "scalar", (1, 1): "split"}
         for z in range(PASSES):
-            picked = [gather_words(side, z) for side in range(2)]
             for side in range(2):
                 name = "w%d_%d" % (side + 1, z)
                 w_mx = mx_tiles(name, H)
-                if side == 1 and z == PASSES - 1:
+                if plan[side, z] == "split":
                     g_lo = interleave(name + "lo", raw_w[side, z], lo, True)
                     g_hi = interleave(name + "hi", raw_w[side, z], hi, False)
                     quantize(w_mx, hi, g_hi)
                     quantize(w_mx, lo, g_lo)
                 else:
-                    quantize(w_mx, whole, interleave(name, raw_w[side, z], whole, True))
-                node_pass(side, z, picked[side], w_mx)
+                    quantize(w_mx, whole, interleave(name, raw_w[side, z], whole, plan[side, z] == "scalar"))
+                node_pass(side, z, picked[side, z], w_mx)
 
         e_mx = [mx_tiles("e%d" % c, EDGE_TILE) for c in range(EDGE_TILES)]
         tile_cols = slice(0, EDGE_TILE)
 
-        def edge_pair(raw, first):
-            grouped = [
-                interleave("e%d" % (first + a), raw, slice(a * EDGE_TILE, (a + 1) * EDGE_TILE), False) for a in range(2)
-            ]
-            for a in range(2):
-                quantize(e_mx[first + a], tile_cols, grouped[a])
-
-        edge_pair(raw_e0, 0)
         w3_mx = mx_tiles("w3", H)
         for a in range(2):
-            quantize(w3_mx, (lo, hi)[a], interleave("w3_%d" % a, raw_w3[a], lo, False))
-        edge_pair(raw_e1, 2)
+            quantize(w3_mx, (lo, hi)[a], interleave("w3_%d" % a, raw_w3[a], lo, a == 0))
+
+        for pair in ((0,), (1, 2), (3,)):
+            grouped = [interleave("e%d" % c, raw_e[c][0], raw_e[c][1], c in ()) for c in pair]
+            for a, c in enumerate(pair):
+                quantize(e_mx[c], tile_cols, grouped[a])
 
         for c in range(EDGE_TILES):
             nc.tensor.matmul_mx(
@@ -167,6 +178,9 @@ def tile_picked_edgeup_gelu_p_kernel(
                 stop=True,
             )
 
+        last = EDGE_TILES - 1
+        out_cols = [h_bank[0][:, c * EDGE_TILE : (c + 1) * EDGE_TILE] for c in range(last)] + [h_bank[last][:, tile_cols]]
+        STORES = {last - 1: (0, slice(0, last * EDGE_TILE)), last: (last, slice(last * EDGE_TILE, V))}
         for c in range(EDGE_TILES):
             h_rows = keep.tile([P, H], BF16, name="h_rows%d" % c, align_bytes=64)
             nc.scalar.activation(
@@ -174,6 +188,7 @@ def tile_picked_edgeup_gelu_p_kernel(
                 in_=h_bank[c][:].rearrange("v (p u e) -> v u p e", u=2, e=2),
                 func=GELU,
             )
+
             pairs = h_rows[:].bitcast(F32)
             for u in range(2):
                 nc.tensor.transpose(t_bank[c][:, u, :], pairs[:, u * P : (u + 1) * P], identity[:])
@@ -185,7 +200,7 @@ def tile_picked_edgeup_gelu_p_kernel(
             h_mx = mx_tiles("h%d" % c, EDGE_TILE)
             quantize(h_mx, tile_cols, h_grouped)
             nc.tensor.matmul_mx(
-                out=h_bank[c][:, tile_cols],
+                out=out_cols[c],
                 lhsT=w4_codes[:].bitcast(FP8X4),
                 lhsT_scale=w4_plane[:],
                 rhs=h_mx[0][:].bitcast(FP8X4),
@@ -193,6 +208,9 @@ def tile_picked_edgeup_gelu_p_kernel(
                 start=True,
                 stop=True,
             )
-            result = keep.tile([P, EDGE_TILE], F32, name="result%d" % c)
-            nc.scalar.copy(out=result[:], in_=h_bank[c][:, tile_cols])
-            nc.sync.dma_start(out=out[:, c * EDGE_TILE : (c + 1) * EDGE_TILE], in_=result[:])
+            if c in STORES:
+                bank, cols = STORES[c]
+                width = cols.stop - cols.start
+                result = keep.tile([P, width], F32, name="result%d" % c)
+                nc.scalar.copy(out=result[:], in_=h_bank[bank][:, 0:width])
+                nc.sync.dma_start(out=out[:, cols], in_=result[:])

@@ -22,7 +22,7 @@ PASSES = K // K_PASS
 EDGE_TILE = 128
 EDGE_TILES = V // EDGE_TILE
 LIST_COL = 16
-E_LOADS = (1, 2, 1)
+E_LOADS = (2, 2)
 
 
 def tile_picked_edgeup_gelu_p_kernel(
@@ -49,6 +49,15 @@ def tile_picked_edgeup_gelu_p_kernel(
                 nc.vector.tensor_copy(out=dst, in_=src)
             return grouped
 
+        def interleave_shared(name, raw, scalar_cols):
+            grouped = keep.tile([P, H * PACK], BF16, name=name + "_grouped", align_bytes=64)
+            for engine, cols in ((nc.scalar.copy, slice(0, scalar_cols)), (nc.vector.tensor_copy, slice(scalar_cols, H))):
+                engine(
+                    out=grouped[:, cols.start * PACK : cols.stop * PACK].rearrange("p (c i j) -> p c j i", i=4, j=PACK),
+                    in_=raw[:, :, cols].rearrange("p j (c i) -> p c j i", i=4),
+                )
+            return grouped
+
         def mx_tiles(name, width):
             codes = keep.tile([P, width], U32, name=name + "_codes", align_bytes=64)
             scales = keep.tile([P, width], U8, name=name + "_scales", align_bytes=64)
@@ -71,11 +80,11 @@ def tile_picked_edgeup_gelu_p_kernel(
         nc.vector.memset(warm[:, 0:1], 0.0)
         nc.scalar.activation(out=warm[:, 1:2], in_=warm[:, 0:1], func=GELU)
 
-        def load_x_scales():
+        def load_x_scales(z):
             for q in range(4):
                 nc.sync.dma_start(
-                    out=x_plane[32 * q : 32 * q + 4 * PASSES, :].bitcast(I32),
-                    in_=x_scales[:, 4 * q : 4 * q + 4, :].bitcast(I32),
+                    out=x_plane[32 * q + 4 * z : 32 * q + 4 * z + 4, :].bitcast(I32),
+                    in_=x_scales[z, 4 * q : 4 * q + 4, :].bitcast(I32),
                 )
 
         def load_w4():
@@ -91,21 +100,22 @@ def tile_picked_edgeup_gelu_p_kernel(
         raw_w = {}
         x_table = {}
         x_table[0] = load_words("x_table0", x_words[0], nc.sync)
-        load_x_scales()
+        load_x_scales(0)
         nc.sync.dma_start(offsets[:], offs)
         raw_w[0, 0] = load_rows("w1_0", w1[0:K_PASS, :])
+        load_x_scales(1)
         x_table[1] = load_words("x_table1", x_words[1], nc.sync)
         raw_w[1, 0] = load_rows("w2_0", w2[0:K_PASS, :])
-        w4_codes = load_w4()
         raw_w[0, 1] = load_rows("w1_1", w1[K_PASS:K, :])
         raw_w[1, 1] = load_rows("w2_1", w2[K_PASS:K, :])
-        raw_w3 = [load_rows("w3_%d" % a, w3[:, a * half : (a + 1) * half]) for a in range(2)]
+        raw_w3 = load_rows("w3", w3)
         raw_e = []
         first = 0
         for tiles in E_LOADS:
             raw = load_rows("e_%d" % first, eT[:, first * EDGE_TILE : (first + tiles) * EDGE_TILE])
             raw_e.extend([(raw, slice(a * EDGE_TILE, (a + 1) * EDGE_TILE)) for a in range(tiles)])
             first = first + tiles
+        w4_codes = load_w4()
 
         identity = keep.tile([P, P], F32, name="identity")
         make_identity(nc, identity[:])
@@ -141,16 +151,13 @@ def tile_picked_edgeup_gelu_p_kernel(
         lo, hi = slice(0, half), slice(half, H)
         gather_plane()
         picked = {(side, z): gather_words(side, z) for z in range(PASSES) for side in range(2)}
-        plan = {(0, 0): "scalar", (1, 0): "scalar", (0, 1): "scalar", (1, 1): "split"}
+        plan = {(0, 0): "scalar", (1, 0): "scalar", (0, 1): "split", (1, 1): "split"}
         for z in range(PASSES):
             for side in range(2):
                 name = "w%d_%d" % (side + 1, z)
                 w_mx = mx_tiles(name, H)
                 if plan[side, z] == "split":
-                    g_lo = interleave(name + "lo", raw_w[side, z], lo, True)
-                    g_hi = interleave(name + "hi", raw_w[side, z], hi, False)
-                    quantize(w_mx, hi, g_hi)
-                    quantize(w_mx, lo, g_lo)
+                    quantize(w_mx, whole, interleave_shared(name, raw_w[side, z], 256))
                 else:
                     quantize(w_mx, whole, interleave(name, raw_w[side, z], whole, plan[side, z] == "scalar"))
                 node_pass(side, z, picked[side, z], w_mx)
@@ -159,11 +166,10 @@ def tile_picked_edgeup_gelu_p_kernel(
         tile_cols = slice(0, EDGE_TILE)
 
         w3_mx = mx_tiles("w3", H)
-        for a in range(2):
-            quantize(w3_mx, (lo, hi)[a], interleave("w3_%d" % a, raw_w3[a], lo, a == 0))
+        quantize(w3_mx, whole, interleave_shared("w3", raw_w3, 160))
 
-        for pair in ((0,), (1, 2), (3,)):
-            grouped = [interleave("e%d" % c, raw_e[c][0], raw_e[c][1], c in ()) for c in pair]
+        for pair in ((0, 1), (2, 3)):
+            grouped = [interleave("e%d" % c, raw_e[c][0], raw_e[c][1], c in (0,)) for c in pair]
             for a, c in enumerate(pair):
                 quantize(e_mx[c], tile_cols, grouped[a])
 

@@ -60,7 +60,7 @@ def tile_picked_edgeup_gelu_p_kernel(
 
         def mx_tiles(name, width):
             codes = keep.tile([P, width], U32, name=name + "_codes", align_bytes=64)
-            scales = keep.tile([P, width], U8, name=name + "_scales", align_bytes=64)
+            scales = keep.tile([P, width], U8, name=name + "_scales", tag=name + "_scales", align_bytes=64)
             return codes, scales
 
         def quantize(mx, cols, grouped):
@@ -72,7 +72,7 @@ def tile_picked_edgeup_gelu_p_kernel(
             return tile
 
         offsets = keep.tile([P, S // LIST_COL], U16, name="offsets")
-        x_plane = keep.tile([P, T], U8, name="x_plane", align_bytes=64)
+        x_plane = keep.tile([P, T], U8, name="x_plane", tag="w1_0_scales", align_bytes=64)
         w4_plane = keep.tile([P, N], U8, name="w4_plane", align_bytes=64)
         nc.vector.memset(x_plane[:].bitcast(I32), 0)
         nc.vector.memset(w4_plane[:].bitcast(I32), 0)
@@ -102,9 +102,9 @@ def tile_picked_edgeup_gelu_p_kernel(
         x_table[0] = load_words("x_table0", x_words[0], nc.sync)
         load_x_scales(0)
         nc.sync.dma_start(offsets[:], offs)
+        x_table[1] = load_words("x_table1", x_words[1], nc.sync)
         raw_w[0, 0] = load_rows("w1_0", w1[0:K_PASS, :])
         load_x_scales(1)
-        x_table[1] = load_words("x_table1", x_words[1], nc.sync)
         raw_w[1, 0] = load_rows("w2_0", w2[0:K_PASS, :])
         raw_w[0, 1] = load_rows("w1_1", w1[K_PASS:K, :])
         raw_w[1, 1] = load_rows("w2_1", w2[K_PASS:K, :])
@@ -149,8 +149,8 @@ def tile_picked_edgeup_gelu_p_kernel(
 
         whole = slice(0, H)
         lo, hi = slice(0, half), slice(half, H)
-        gather_plane()
         picked = {(side, z): gather_words(side, z) for z in range(PASSES) for side in range(2)}
+        gather_plane()
         plan = {(0, 0): "scalar", (1, 0): "scalar", (0, 1): "split", (1, 1): "split"}
         for z in range(PASSES):
             for side in range(2):
@@ -185,8 +185,8 @@ def tile_picked_edgeup_gelu_p_kernel(
             )
 
         last = EDGE_TILES - 1
-        out_cols = [h_bank[0][:, c * EDGE_TILE : (c + 1) * EDGE_TILE] for c in range(last)] + [h_bank[last][:, tile_cols]]
-        STORES = {last - 1: (0, slice(0, last * EDGE_TILE)), last: (last, slice(last * EDGE_TILE, V))}
+        out_cols = [h_bank[0][:, 0:128], h_bank[0][:, 128:256], h_bank[2][:, tile_cols], h_bank[3][:, tile_cols]]
+        STORES = {1: (0, slice(0, 256)), 2: (2, slice(256, 384)), 3: (3, slice(384, 512))}
         for c in range(EDGE_TILES):
             h_rows = keep.tile([P, H], BF16, name="h_rows%d" % c, align_bytes=64)
             nc.scalar.activation(

@@ -1,7 +1,6 @@
 from contextlib import ExitStack
 
 import concourse.mybir as mybir
-from concourse.masks import make_identity
 
 K, T, S, V, H, N, J = 1024, 2048, 1024, 512, 512, 128, 512
 FLOPS = 2 * V * H * (2 * K + J) + 2 * V * H * N
@@ -22,7 +21,6 @@ PASSES = K // K_PASS
 EDGE_TILE = 128
 EDGE_TILES = V // EDGE_TILE
 LIST_COL = 16
-E_LOADS = (2, 2)
 
 
 def tile_picked_edgeup_gelu_p_kernel(
@@ -31,6 +29,7 @@ def tile_picked_edgeup_gelu_p_kernel(
     nc = tc.nc
     with ExitStack() as ctx:
         keep = ctx.enter_context(tc.tile_pool(name="keep", bufs=1))
+        reuse = ctx.enter_context(tc.tile_pool(name="reuse", bufs=1))
         psum = ctx.enter_context(tc.psum_pool(name="psum", bufs=1))
 
         def load_rows(name, rows):
@@ -38,41 +37,44 @@ def tile_picked_edgeup_gelu_p_kernel(
             nc.sync.dma_start(out=raw[:], in_=rows.rearrange("(p j) c -> p j c", j=PACK))
             return raw
 
-        def interleave(name, raw, cols, on_scalar):
-            width = cols.stop - cols.start
-            grouped = keep.tile([P, width * PACK], BF16, name=name + "_grouped", align_bytes=64)
-            dst = grouped[:].rearrange("p (c i j) -> p c j i", i=4, j=PACK)
-            src = raw[:, :, cols].rearrange("p j (c i) -> p c j i", i=4)
-            if on_scalar:
-                nc.scalar.copy(out=dst, in_=src)
-            else:
-                nc.vector.tensor_copy(out=dst, in_=src)
-            return grouped
-
-        def interleave_shared(name, raw, scalar_cols):
-            grouped = keep.tile([P, H * PACK], BF16, name=name + "_grouped", align_bytes=64)
-            for engine, cols in ((nc.scalar.copy, slice(0, scalar_cols)), (nc.vector.tensor_copy, slice(scalar_cols, H))):
-                engine(
-                    out=grouped[:, cols.start * PACK : cols.stop * PACK].rearrange("p (c i j) -> p c j i", i=4, j=PACK),
-                    in_=raw[:, :, cols].rearrange("p j (c i) -> p c j i", i=4),
-                )
-            return grouped
-
-        def mx_tiles(name, width):
-            codes = keep.tile([P, width], U32, name=name + "_codes", align_bytes=64)
-            scales = keep.tile([P, width], U8, name=name + "_scales", tag=name + "_scales", align_bytes=64)
-            return codes, scales
-
-        def quantize(mx, cols, grouped):
-            nc.vector.quantize_mx(out=mx[0][:, cols].bitcast(FP8X4), scales=mx[1][:, cols], in_=grouped[:])
-
-        def load_words(name, words, queue):
+        def load_words(name, words):
             tile = keep.tile([P, words.shape[1]], U32, name=name, align_bytes=64)
-            queue.dma_start(out=tile[:].bitcast(I32), in_=words.rearrange("p n t -> p (n t)").bitcast(I32))
+            nc.sync.dma_start(out=tile[:].bitcast(I32), in_=words.rearrange("p n t -> p (n t)").bitcast(I32))
             return tile
 
+        def load_scale_rows(plane, first, rows, r):
+            nc.sync.dma_start(out=plane[first + r : P : 32, :].bitcast(I32), in_=rows[r : 16 : 4, :].bitcast(I32))
+
+        def round_weights(name, raw, half, copy):
+            grouped = keep.tile([P, H * PACK // 2], BF16, name="%s_grouped%d" % (name, half), align_bytes=64)
+            copy(
+                out=grouped[:].rearrange("p (t m j) -> p m j t", t=2, j=PACK),
+                in_=raw[:].rearrange("p j (m t) -> p m j t", t=PACK)[:, :, :, 2 * half : 2 * half + 2],
+            )
+            return grouped
+
+        def weights_mx(name, raw, copies, planes=(None, None)):
+            grouped = [round_weights(name, raw, half, copies[half]) for half in range(2)]
+            return [quantize("%s_%d" % (name, half), grouped[half], planes[half]) for half in range(2)]
+
+        def round_edges(name, raw, copy):
+            grouped = keep.tile([P, EDGE_TILE * PACK], BF16, name=name + "_grouped", align_bytes=64)
+            copy(
+                out=grouped[:].rearrange("p (c i j) -> p c j i", i=4, j=PACK),
+                in_=raw[:].rearrange("p j (c i) -> p c j i", i=4),
+            )
+            return grouped
+
+        def quantize(name, grouped, scales=None):
+            width = grouped.shape[1] // PACK
+            codes = keep.tile([P, width], U32, name=name + "_codes", align_bytes=64)
+            if scales is None:
+                scales = keep.tile([P, width], U8, name=name + "_scales", align_bytes=64)
+            nc.vector.quantize_mx(out=codes[:].bitcast(FP8X4), scales=scales[:], in_=grouped[:])
+            return codes, scales
+
         offsets = keep.tile([P, S // LIST_COL], U16, name="offsets")
-        x_plane = keep.tile([P, T], U8, name="x_plane", tag="w1_0_scales", align_bytes=64)
+        x_plane = reuse.tile([P, T], U8, name="x_plane", align_bytes=64, offset=0)
         w4_plane = keep.tile([P, N], U8, name="w4_plane", align_bytes=64)
         nc.vector.memset(x_plane[:].bitcast(I32), 0)
         nc.vector.memset(w4_plane[:].bitcast(I32), 0)
@@ -80,133 +82,83 @@ def tile_picked_edgeup_gelu_p_kernel(
         nc.vector.memset(warm[:, 0:1], 0.0)
         nc.scalar.activation(out=warm[:, 1:2], in_=warm[:, 0:1], func=GELU)
 
-        def load_x_scales(z):
-            for q in range(4):
-                nc.sync.dma_start(
-                    out=x_plane[32 * q + 4 * z : 32 * q + 4 * z + 4, :].bitcast(I32),
-                    in_=x_scales[z, 4 * q : 4 * q + 4, :].bitcast(I32),
-                )
-
-        def load_w4():
-            codes = load_words("w4_codes", w4_words[0], nc.sync)
-            for q in range(4):
-                nc.sync.dma_start(
-                    out=w4_plane[32 * q : 32 * q + 4, :].bitcast(I32),
-                    in_=w4_scales[0, 4 * q : 4 * q + 4, :].bitcast(I32),
-                )
-            return codes
-
-        half = V // 2
         raw_w = {}
         x_table = {}
-        x_table[0] = load_words("x_table0", x_words[0], nc.sync)
-        load_x_scales(0)
         nc.sync.dma_start(offsets[:], offs)
-        x_table[1] = load_words("x_table1", x_words[1], nc.sync)
+        x_table[0] = load_words("x_table0", x_words[0])
+        for r in (0, 1):
+            for z in range(PASSES):
+                load_scale_rows(x_plane, 4 * z, x_scales[z], r)
         raw_w[0, 0] = load_rows("w1_0", w1[0:K_PASS, :])
-        load_x_scales(1)
+        for r in (2, 3):
+            for z in range(PASSES):
+                load_scale_rows(x_plane, 4 * z, x_scales[z], r)
+        x_table[1] = load_words("x_table1", x_words[1])
         raw_w[1, 0] = load_rows("w2_0", w2[0:K_PASS, :])
         raw_w[0, 1] = load_rows("w1_1", w1[K_PASS:K, :])
         raw_w[1, 1] = load_rows("w2_1", w2[K_PASS:K, :])
         raw_w3 = load_rows("w3", w3)
-        raw_e = []
-        first = 0
-        for tiles in E_LOADS:
-            raw = load_rows("e_%d" % first, eT[:, first * EDGE_TILE : (first + tiles) * EDGE_TILE])
-            raw_e.extend([(raw, slice(a * EDGE_TILE, (a + 1) * EDGE_TILE)) for a in range(tiles)])
-            first = first + tiles
-        w4_codes = load_w4()
+        raw_e = [load_rows("e%d" % c, eT[:, c * EDGE_TILE : (c + 1) * EDGE_TILE]) for c in range(EDGE_TILES)]
+        w4_codes = load_words("w4_codes", w4_words[0])
+        for r in range(4):
+            load_scale_rows(w4_plane, 0, w4_scales[0], r)
 
-        identity = keep.tile([P, P], F32, name="identity")
-        make_identity(nc, identity[:])
+        h_bank = [psum.tile([P, PACK, EDGE_TILE], F32, name="h_bank%d" % c) for c in range(EDGE_TILES)]
+        out_bank = [psum.tile([P, V], F32, name="out_bank%d" % c) for c in range(EDGE_TILES)]
 
-        h_bank = [psum.tile([P, H], F32, name="h_bank%d" % c) for c in range(EDGE_TILES)]
-        t_bank = [psum.tile([P, 2, EDGE_TILE], F32, name="t_bank%d" % c) for c in range(EDGE_TILES)]
-
-        picked_plane = keep.tile([P, S], U8, name="picked_plane", align_bytes=64)
-
-        def gather_plane():
-            nc.vector.tensor_copy(picked_plane[:], x_plane[:].indirect(offsets[:]))
-
-        def gather_words(side, z):
-            picked = keep.tile([P, V], U32, name="picked%d_%d" % (side, z), align_bytes=64)
-            cols = slice(side * V // LIST_COL, (side + 1) * V // LIST_COL)
-            nc.vector.tensor_copy(picked[:], x_table[z][:].indirect(offsets[:, cols]))
+        def gather_words(z, picked):
+            nc.vector.tensor_copy(picked[:], x_table[z][:].indirect(offsets[:]))
             return picked
+
+        def hidden_pass(c, w_mx, codes, scales, first, last):
+            for t in range(PACK):
+                cols = slice(t % 2 * P, (t % 2 + 1) * P)
+                nc.tensor.matmul_mx(
+                    out=h_bank[c][:, t, :],
+                    lhsT=w_mx[t // 2][0][:, cols].bitcast(FP8X4),
+                    lhsT_scale=w_mx[t // 2][1][:, cols],
+                    rhs=codes.bitcast(FP8X4),
+                    rhs_scale=scales,
+                    start=(first and t == 0),
+                    stop=(last and t == PACK - 1),
+                )
 
         def node_pass(side, z, picked, w_mx):
             for c in range(EDGE_TILES):
-                e0 = c * EDGE_TILE
-                nc.tensor.matmul_mx(
-                    out=h_bank[c][:],
-                    lhsT=picked[:, e0 : e0 + EDGE_TILE].bitcast(FP8X4),
-                    lhsT_scale=picked_plane[4 * z : P, side * V + e0 : side * V + e0 + EDGE_TILE],
-                    rhs=w_mx[0][:].bitcast(FP8X4),
-                    rhs_scale=w_mx[1][:],
-                    start=(side == 0 and z == 0),
-                    stop=False,
-                )
+                cols = slice(side * V + c * EDGE_TILE, side * V + (c + 1) * EDGE_TILE)
+                hidden_pass(c, w_mx, picked[:, cols], picked_plane[4 * z : P, cols], side == 0 and z == 0, False)
 
-        whole = slice(0, H)
-        lo, hi = slice(0, half), slice(half, H)
-        picked = {(side, z): gather_words(side, z) for z in range(PASSES) for side in range(2)}
-        gather_plane()
-        plan = {(0, 0): "scalar", (1, 0): "scalar", (0, 1): "split", (1, 1): "split"}
-        for z in range(PASSES):
-            for side in range(2):
-                name = "w%d_%d" % (side + 1, z)
-                w_mx = mx_tiles(name, H)
-                if plan[side, z] == "split":
-                    quantize(w_mx, whole, interleave_shared(name, raw_w[side, z], 256))
-                else:
-                    quantize(w_mx, whole, interleave(name, raw_w[side, z], whole, plan[side, z] == "scalar"))
-                node_pass(side, z, picked[side, z], w_mx)
-
-        e_mx = [mx_tiles("e%d" % c, EDGE_TILE) for c in range(EDGE_TILES)]
-        tile_cols = slice(0, EDGE_TILE)
-
-        w3_mx = mx_tiles("w3", H)
-        quantize(w3_mx, whole, interleave_shared("w3", raw_w3, 160))
-
-        for pair in ((0, 1), (2, 3)):
-            grouped = [interleave("e%d" % c, raw_e[c][0], raw_e[c][1], c in (0,)) for c in pair]
-            for a, c in enumerate(pair):
-                quantize(e_mx[c], tile_cols, grouped[a])
+        picked_plane = keep.tile([P, S], U8, name="picked_plane", align_bytes=64)
+        w_mx = {}
+        picked = {}
+        picked[0] = gather_words(0, keep.tile([P, S], U32, name="picked0", align_bytes=64))
+        nc.vector.tensor_copy(picked_plane[:], x_plane[:].indirect(offsets[:]))
+        planes = [reuse.tile([P, H // 2], U8, name="w1_0_scales%d" % a, align_bytes=64, offset=a * H // 2) for a in range(2)]
+        w_mx[0, 0] = weights_mx("w1_0", raw_w[0, 0], (nc.scalar.copy, nc.scalar.copy), planes)
+        shared = (nc.vector.tensor_copy, nc.scalar.copy)
+        picked[1] = gather_words(1, reuse.tile([P, S], U32, name="picked1", align_bytes=64, offset=H))
+        node_pass(0, 0, picked[0], w_mx[0, 0])
+        for side, z in ((1, 0), (0, 1), (1, 1)):
+            name = "w%d_%d" % (side + 1, z)
+            w_mx[side, z] = weights_mx(name, raw_w[side, z], shared)
+            node_pass(side, z, picked[z], w_mx[side, z])
+        w3_mx = weights_mx("w3", raw_w3, shared)
 
         for c in range(EDGE_TILES):
-            nc.tensor.matmul_mx(
-                out=h_bank[c][:],
-                lhsT=e_mx[c][0][:].bitcast(FP8X4),
-                lhsT_scale=e_mx[c][1][:],
-                rhs=w3_mx[0][:].bitcast(FP8X4),
-                rhs_scale=w3_mx[1][:],
-                start=False,
-                stop=True,
-            )
+            copy = nc.scalar.copy if c == 1 else nc.vector.tensor_copy
+            e_mx = quantize("e%d" % c, round_edges("e%d" % c, raw_e[c], copy))
+            hidden_pass(c, w3_mx, e_mx[0][:], e_mx[1][:], False, True)
 
-        last = EDGE_TILES - 1
-        out_cols = [h_bank[0][:, 0:128], h_bank[0][:, 128:256], h_bank[2][:, tile_cols], h_bank[3][:, tile_cols]]
-        STORES = {1: (0, slice(0, 256)), 2: (2, slice(256, 384)), 3: (3, slice(384, 512))}
         for c in range(EDGE_TILES):
-            h_rows = keep.tile([P, H], BF16, name="h_rows%d" % c, align_bytes=64)
+            h_grouped = keep.tile([P, EDGE_TILE * PACK], BF16, name="h_grouped%d" % c, align_bytes=64)
             nc.scalar.activation(
-                out=h_rows[:].rearrange("v (u p e) -> v u p e", u=2, e=2),
-                in_=h_bank[c][:].rearrange("v (p u e) -> v u p e", u=2, e=2),
+                out=h_grouped[:].rearrange("p (v t) -> p v t", t=PACK),
+                in_=h_bank[c][:].rearrange("p t v -> p v t"),
                 func=GELU,
             )
-
-            pairs = h_rows[:].bitcast(F32)
-            for u in range(2):
-                nc.tensor.transpose(t_bank[c][:, u, :], pairs[:, u * P : (u + 1) * P], identity[:])
-            h_grouped = keep.tile([P, EDGE_TILE * PACK], BF16, name="h_grouped%d" % c, align_bytes=64)
-            nc.vector.tensor_copy(
-                out=h_grouped[:].bitcast(F32).rearrange("p (v u) -> p v u", u=2),
-                in_=t_bank[c][:].rearrange("p u v -> p v u"),
-            )
-            h_mx = mx_tiles("h%d" % c, EDGE_TILE)
-            quantize(h_mx, tile_cols, h_grouped)
+            h_mx = quantize("h%d" % c, h_grouped)
             nc.tensor.matmul_mx(
-                out=out_cols[c],
+                out=out_bank[c][:, 0:EDGE_TILE],
                 lhsT=w4_codes[:].bitcast(FP8X4),
                 lhsT_scale=w4_plane[:],
                 rhs=h_mx[0][:].bitcast(FP8X4),
@@ -214,9 +166,6 @@ def tile_picked_edgeup_gelu_p_kernel(
                 start=True,
                 stop=True,
             )
-            if c in STORES:
-                bank, cols = STORES[c]
-                width = cols.stop - cols.start
-                result = keep.tile([P, width], F32, name="result%d" % c)
-                nc.scalar.copy(out=result[:], in_=h_bank[bank][:, 0:width])
-                nc.sync.dma_start(out=out[:, cols], in_=result[:])
+            result = keep.tile([P, EDGE_TILE], F32, name="result%d" % c)
+            nc.vector.tensor_copy(out=result[:], in_=out_bank[c][:, 0:EDGE_TILE])
+            nc.sync.dma_start(out=out[:, c * EDGE_TILE : (c + 1) * EDGE_TILE], in_=result[:])

@@ -45,16 +45,13 @@ def tile_picked_edgeup_gelu_p_kernel(
         def load_scale_rows(plane, first, rows, r):
             nc.sync.dma_start(out=plane[first + r : P : 32, :].bitcast(I32), in_=rows[r : 16 : 4, :].bitcast(I32))
 
-        def round_weights(name, raw, half, copy):
-            grouped = keep.tile([P, H * PACK // 2], BF16, name="%s_grouped%d" % (name, half), align_bytes=64)
-            copy(
-                out=grouped[:].rearrange("p (t m j) -> p m j t", t=2, j=PACK),
-                in_=raw[:].rearrange("p j (m t) -> p m j t", t=PACK)[:, :, :, 2 * half : 2 * half + 2],
-            )
-            return grouped
-
         def weights_mx(name, raw, copies, planes=(None, None)):
-            grouped = [round_weights(name, raw, half, copies[half]) for half in range(2)]
+            grouped = [keep.tile([P, H * PACK // 2], BF16, name="%s_grouped%d" % (name, half), align_bytes=64) for half in range(2)]
+            for half in range(2):
+                copies[half](
+                    out=grouped[half][:].rearrange("p (t m j) -> p m j t", t=2, j=PACK),
+                    in_=raw[:].rearrange("p j (m t) -> p m j t", t=PACK)[:, :, :, 2 * half : 2 * half + 2],
+                )
             return [quantize("%s_%d" % (name, half), grouped[half], planes[half]) for half in range(2)]
 
         def round_edges(name, raw, copy):
@@ -89,11 +86,11 @@ def tile_picked_edgeup_gelu_p_kernel(
         for r in (0, 1):
             for z in range(PASSES):
                 load_scale_rows(x_plane, 4 * z, x_scales[z], r)
+        x_table[1] = load_words("x_table1", x_words[1])
         raw_w[0, 0] = load_rows("w1_0", w1[0:K_PASS, :])
         for r in (2, 3):
             for z in range(PASSES):
                 load_scale_rows(x_plane, 4 * z, x_scales[z], r)
-        x_table[1] = load_words("x_table1", x_words[1])
         raw_w[1, 0] = load_rows("w2_0", w2[0:K_PASS, :])
         raw_w[0, 1] = load_rows("w1_1", w1[K_PASS:K, :])
         raw_w[1, 1] = load_rows("w2_1", w2[K_PASS:K, :])
@@ -131,12 +128,12 @@ def tile_picked_edgeup_gelu_p_kernel(
         picked_plane = keep.tile([P, S], U8, name="picked_plane", align_bytes=64)
         w_mx = {}
         picked = {}
-        picked[0] = gather_words(0, keep.tile([P, S], U32, name="picked0", align_bytes=64))
+        for z in range(PASSES):
+            picked[z] = gather_words(z, keep.tile([P, S], U32, name="picked%d" % z, align_bytes=64))
         nc.vector.tensor_copy(picked_plane[:], x_plane[:].indirect(offsets[:]))
         planes = [reuse.tile([P, H // 2], U8, name="w1_0_scales%d" % a, align_bytes=64, offset=a * H // 2) for a in range(2)]
         w_mx[0, 0] = weights_mx("w1_0", raw_w[0, 0], (nc.scalar.copy, nc.scalar.copy), planes)
         shared = (nc.vector.tensor_copy, nc.scalar.copy)
-        picked[1] = gather_words(1, reuse.tile([P, S], U32, name="picked1", align_bytes=64, offset=H))
         node_pass(0, 0, picked[0], w_mx[0, 0])
         for side, z in ((1, 0), (0, 1), (1, 1)):
             name = "w%d_%d" % (side + 1, z)
@@ -149,7 +146,7 @@ def tile_picked_edgeup_gelu_p_kernel(
             e_mx = quantize("e%d" % c, round_edges("e%d" % c, raw_e[c], copy))
             hidden_pass(c, w3_mx, e_mx[0][:], e_mx[1][:], False, True)
 
-        for c in range(EDGE_TILES):
+        def second_product(c):
             h_grouped = keep.tile([P, EDGE_TILE * PACK], BF16, name="h_grouped%d" % c, align_bytes=64)
             nc.scalar.activation(
                 out=h_grouped[:].rearrange("p (v t) -> p v t", t=PACK),
@@ -166,6 +163,14 @@ def tile_picked_edgeup_gelu_p_kernel(
                 start=True,
                 stop=True,
             )
+
+        def store(c):
             result = keep.tile([P, EDGE_TILE], F32, name="result%d" % c)
             nc.vector.tensor_copy(out=result[:], in_=out_bank[c][:, 0:EDGE_TILE])
             nc.sync.dma_start(out=out[:, c * EDGE_TILE : (c + 1) * EDGE_TILE], in_=result[:])
+
+        for c in range(EDGE_TILES + 1):
+            if c < EDGE_TILES:
+                second_product(c)
+            if c > 0:
+                store(c - 1)

@@ -58,7 +58,7 @@ def tile_picked_edgeup_gelu_p_kernel(
             grouped = keep.tile([P, EDGE_TILE * PACK], BF16, name=name + "_grouped", align_bytes=64)
             copy(
                 out=grouped[:].rearrange("p (c i j) -> p c j i", i=4, j=PACK),
-                in_=raw[:].rearrange("p j (c i) -> p c j i", i=4),
+                in_=raw.rearrange("p j (c i) -> p c j i", i=4),
             )
             return grouped
 
@@ -95,7 +95,10 @@ def tile_picked_edgeup_gelu_p_kernel(
         raw_w[0, 1] = load_rows("w1_1", w1[K_PASS:K, :])
         raw_w[1, 1] = load_rows("w2_1", w2[K_PASS:K, :])
         raw_w3 = load_rows("w3", w3)
-        raw_e = [load_rows("e%d" % c, eT[:, c * EDGE_TILE : (c + 1) * EDGE_TILE]) for c in range(EDGE_TILES)]
+        raw_e = []
+        for a in range(2):
+            raw = load_rows("e%d" % a, eT[:, a * V // 2 : (a + 1) * V // 2])
+            raw_e.extend([raw[:, :, 0:EDGE_TILE], raw[:, :, EDGE_TILE : 2 * EDGE_TILE]])
         w4_codes = load_words("w4_codes", w4_words[0])
         for r in range(4):
             load_scale_rows(w4_plane, 0, w4_scales[0], r)

@@ -21,6 +21,7 @@ PASSES = K // K_PASS
 EDGE_TILE = 128
 EDGE_TILES = V // EDGE_TILE
 LIST_COL = 16
+E_LOADS = (2, 1, 1)
 
 
 def tile_picked_edgeup_gelu_p_kernel(
@@ -96,9 +97,10 @@ def tile_picked_edgeup_gelu_p_kernel(
         raw_w[1, 1] = load_rows("w2_1", w2[K_PASS:K, :])
         raw_w3 = load_rows("w3", w3)
         raw_e = []
-        for a in range(2):
-            raw = load_rows("e%d" % a, eT[:, a * V // 2 : (a + 1) * V // 2])
-            raw_e.extend([raw[:, :, 0:EDGE_TILE], raw[:, :, EDGE_TILE : 2 * EDGE_TILE]])
+        for tiles in E_LOADS:
+            first = len(raw_e) * EDGE_TILE
+            raw = load_rows("e%d" % first, eT[:, first : first + tiles * EDGE_TILE])
+            raw_e.extend([raw[:, :, a * EDGE_TILE : (a + 1) * EDGE_TILE] for a in range(tiles)])
         w4_codes = load_words("w4_codes", w4_words[0])
         for r in range(4):
             load_scale_rows(w4_plane, 0, w4_scales[0], r)

@@ -31,6 +31,7 @@ def tile_picked_edgeup_gelu_p_kernel(
     with ExitStack() as ctx:
         keep = ctx.enter_context(tc.tile_pool(name="keep", bufs=1))
         reuse = ctx.enter_context(tc.tile_pool(name="reuse", bufs=1))
+        pair = ctx.enter_context(tc.tile_pool(name="pair", bufs=2))
         psum = ctx.enter_context(tc.psum_pool(name="psum", bufs=1))
 
         def load_rows(name, rows):
@@ -158,7 +159,10 @@ def tile_picked_edgeup_gelu_p_kernel(
                 in_=h_bank[c][:].rearrange("p t v -> p v t"),
                 func=GELU,
             )
-            h_mx = quantize("h%d" % c, h_grouped)
+            h_codes = pair.tile([P, EDGE_TILE], U32, name="h_codes", align_bytes=64)
+            h_scales = pair.tile([P, EDGE_TILE], U8, name="h_scales", align_bytes=64)
+            nc.vector.quantize_mx(out=h_codes[:].bitcast(FP8X4), scales=h_scales[:], in_=h_grouped[:])
+            h_mx = (h_codes, h_scales)
             nc.tensor.matmul_mx(
                 out=out_bank[c][:, 0:EDGE_TILE],
                 lhsT=w4_codes[:].bitcast(FP8X4),

@@ -143,7 +143,7 @@ def tile_picked_edgeup_gelu_p_kernel(
         node_pass(0, 0, picked[0], w_mx[0, 0])
         for side, z in ((1, 0), (0, 1), (1, 1)):
             name = "w%d_%d" % (side + 1, z)
-            w_mx[side, z] = weights_mx(name, raw_w[side, z], shared)
+            w_mx[side, z] = weights_mx(name, raw_w[side, z], shared if z else (nc.scalar.copy, nc.scalar.copy))
             node_pass(side, z, picked[z], w_mx[side, z])
         w3_mx = weights_mx("w3", raw_w3, shared)
 

@@ -83,8 +83,8 @@ def tile_picked_edgeup_gelu_p_kernel(
 
         raw_w = {}
         x_table = {}
-        nc.sync.dma_start(offsets[:], offs)
         x_table[0] = load_words("x_table0", x_words[0])
+        nc.sync.dma_start(offsets[:], offs)
         for r in (0, 1):
             for z in range(PASSES):
                 load_scale_rows(x_plane, 4 * z, x_scales[z], r)

@@ -35,12 +35,12 @@ def tile_picked_edgeup_gelu_p_kernel(
         psum = ctx.enter_context(tc.psum_pool(name="psum", bufs=1))
 
         def load_rows(name, rows):
-            raw = keep.tile([P, PACK, rows.shape[1]], F32, name=name + "_raw")
+            raw = keep.tile([P, PACK, rows.shape[1]], F32, name=name + "_raw", align_bytes=256)
             nc.sync.dma_start(out=raw[:], in_=rows.rearrange("(p j) c -> p j c", j=PACK))
             return raw
 
         def load_words(name, words):
-            tile = keep.tile([P, words.shape[1]], U32, name=name, align_bytes=64)
+            tile = keep.tile([P, words.shape[1]], U32, name=name, align_bytes=256)
             nc.sync.dma_start(out=tile[:].bitcast(I32), in_=words.rearrange("p n t -> p (n t)").bitcast(I32))
             return tile
 
@@ -72,9 +72,9 @@ def tile_picked_edgeup_gelu_p_kernel(
             nc.vector.quantize_mx(out=codes[:].bitcast(FP8X4), scales=scales[:], in_=grouped[:])
             return codes, scales
 
-        offsets = keep.tile([P, S // LIST_COL], U16, name="offsets")
-        x_plane = reuse.tile([P, T], U8, name="x_plane", align_bytes=64, offset=0)
-        w4_plane = keep.tile([P, N], U8, name="w4_plane", align_bytes=64)
+        offsets = keep.tile([P, S // LIST_COL], U16, name="offsets", align_bytes=256)
+        x_plane = reuse.tile([P, T], U8, name="x_plane", align_bytes=256, offset=0)
+        w4_plane = keep.tile([P, N], U8, name="w4_plane", align_bytes=256)
         nc.vector.memset(x_plane[:].bitcast(I32), 0)
         nc.vector.memset(w4_plane[:].bitcast(I32), 0)
         warm = keep.tile([P, 2], F32, name="warm")
@@ -174,7 +174,7 @@ def tile_picked_edgeup_gelu_p_kernel(
             )
 
         def store(c):
-            result = keep.tile([P, EDGE_TILE], F32, name="result%d" % c)
+            result = keep.tile([P, EDGE_TILE], F32, name="result%d" % c, align_bytes=256)
             nc.vector.tensor_copy(out=result[:], in_=out_bank[c][:, 0:EDGE_TILE])
             nc.sync.dma_start(out=out[:, c * EDGE_TILE : (c + 1) * EDGE_TILE], in_=result[:])
 

@@ -22,6 +22,7 @@ EDGE_TILE = 128
 EDGE_TILES = V // EDGE_TILE
 LIST_COL = 16
 E_LOADS = (2, 1, 1)
+VECTOR_EDGES = (128, 0, 128, 88)
 
 
 def tile_picked_edgeup_gelu_p_kernel(
@@ -56,12 +57,14 @@ def tile_picked_edgeup_gelu_p_kernel(
                 )
             return [quantize("%s_%d" % (name, half), grouped[half], planes[half]) for half in range(2)]
 
-        def round_edges(name, raw, copy):
+        def round_edges(name, raw, on_vector):
             grouped = keep.tile([P, EDGE_TILE * PACK], BF16, name=name + "_grouped", align_bytes=64)
-            copy(
-                out=grouped[:].rearrange("p (c i j) -> p c j i", i=4, j=PACK),
-                in_=raw.rearrange("p j (c i) -> p c j i", i=4),
-            )
+            for copy, first, last in ((nc.vector.tensor_copy, 0, on_vector), (nc.scalar.copy, on_vector, EDGE_TILE)):
+                if last > first:
+                    copy(
+                        out=grouped[:, first * PACK : last * PACK].rearrange("p (c i j) -> p c j i", i=4, j=PACK),
+                        in_=raw[:, :, first:last].rearrange("p j (c i) -> p c j i", i=4),
+                    )
             return grouped
 
         def quantize(name, grouped, scales=None):
@@ -148,8 +151,7 @@ def tile_picked_edgeup_gelu_p_kernel(
         w3_mx = weights_mx("w3", raw_w3, shared)
 
         for c in range(EDGE_TILES):
-            copy = nc.scalar.copy if c == 1 else nc.vector.tensor_copy
-            e_mx = quantize("e%d" % c, round_edges("e%d" % c, raw_e[c], copy))
+            e_mx = quantize("e%d" % c, round_edges("e%d" % c, raw_e[c], VECTOR_EDGES[c]))
             hidden_pass(c, w3_mx, e_mx[0][:], e_mx[1][:], False, True)
 
         def second_product(c):

from contextlib import ExitStack

import concourse.mybir as mybir

K, T, S, V, H, N, J = 1024, 2048, 1024, 512, 512, 128, 512
FLOPS = 2 * V * H * (2 * K + J) + 2 * V * H * N

F32 = mybir.dt.float32
BF16 = mybir.dt.bfloat16
I32 = mybir.dt.int32
U32 = mybir.dt.uint32
U16 = mybir.dt.uint16
U8 = mybir.dt.uint8
FP8X4 = mybir.dt.float8_e4m3fn_x4
GELU = mybir.ActivationFunctionType.Gelu_apprx_tanh

P = 128
PACK = 4
K_PASS = P * PACK
PASSES = K // K_PASS
EDGE_TILE = 128
EDGE_TILES = V // EDGE_TILE
LIST_COL = 16
E_LOADS = (2, 1, 1)
VECTOR_EDGES = (128, 0, 128, 88)


def tile_picked_edgeup_gelu_p_kernel(
    tc, x_words, x_scales, eT, w1, w2, w3, w4_words, w4_scales, offs, out
):
    nc = tc.nc
    with ExitStack() as ctx:
        keep = ctx.enter_context(tc.tile_pool(name="keep", bufs=1))
        reuse = ctx.enter_context(tc.tile_pool(name="reuse", bufs=1))
        pair = ctx.enter_context(tc.tile_pool(name="pair", bufs=2))
        psum = ctx.enter_context(tc.psum_pool(name="psum", bufs=1))

        def load_rows(name, rows):
            raw = keep.tile([P, PACK, rows.shape[1]], F32, name=name + "_raw", align_bytes=256)
            nc.sync.dma_start(out=raw[:], in_=rows.rearrange("(p j) c -> p j c", j=PACK))
            return raw

        def load_words(name, words):
            tile = keep.tile([P, words.shape[1]], U32, name=name, align_bytes=256)
            nc.sync.dma_start(out=tile[:].bitcast(I32), in_=words.rearrange("p n t -> p (n t)").bitcast(I32))
            return tile

        def load_scale_rows(plane, first, rows, r):
            nc.sync.dma_start(out=plane[first + r : P : 32, :].bitcast(I32), in_=rows[r : 16 : 4, :].bitcast(I32))

        def weights_mx(name, raw, copies, planes=(None, None)):
            grouped = [keep.tile([P, H * PACK // 2], BF16, name="%s_grouped%d" % (name, half), align_bytes=64) for half in range(2)]
            for half in range(2):
                copies[half](
                    out=grouped[half][:].rearrange("p (t m j) -> p m j t", t=2, j=PACK),
                    in_=raw[:].rearrange("p j (m t) -> p m j t", t=PACK)[:, :, :, 2 * half : 2 * half + 2],
                )
            return [quantize("%s_%d" % (name, half), grouped[half], planes[half]) for half in range(2)]

        def round_edges(name, raw, on_vector):
            grouped = keep.tile([P, EDGE_TILE * PACK], BF16, name=name + "_grouped", align_bytes=64)
            for copy, first, last in ((nc.vector.tensor_copy, 0, on_vector), (nc.scalar.copy, on_vector, EDGE_TILE)):
                if last > first:
                    copy(
                        out=grouped[:, first * PACK : last * PACK].rearrange("p (c i j) -> p c j i", i=4, j=PACK),
                        in_=raw[:, :, first:last].rearrange("p j (c i) -> p c j i", i=4),
                    )
            return grouped

        def quantize(name, grouped, scales=None):
            width = grouped.shape[1] // PACK
            codes = keep.tile([P, width], U32, name=name + "_codes", align_bytes=64)
            if scales is None:
                scales = keep.tile([P, width], U8, name=name + "_scales", align_bytes=64)
            nc.vector.quantize_mx(out=codes[:].bitcast(FP8X4), scales=scales[:], in_=grouped[:])
            return codes, scales

        offsets = keep.tile([P, S // LIST_COL], U16, name="offsets", align_bytes=256)
        x_plane = reuse.tile([P, T], U8, name="x_plane", align_bytes=256, offset=0)
        w4_plane = keep.tile([P, N], U8, name="w4_plane", align_bytes=256)
        nc.vector.memset(x_plane[:].bitcast(I32), 0)
        nc.vector.memset(w4_plane[:].bitcast(I32), 0)
        warm = keep.tile([P, 2], F32, name="warm")
        nc.vector.memset(warm[:, 0:1], 0.0)
        nc.scalar.activation(out=warm[:, 1:2], in_=warm[:, 0:1], func=GELU)

        raw_w = {}
        x_table = {}
        x_table[0] = load_words("x_table0", x_words[0])
        nc.sync.dma_start(offsets[:], offs)
        for r in (0, 1):
            for z in range(PASSES):
                load_scale_rows(x_plane, 4 * z, x_scales[z], r)
        x_table[1] = load_words("x_table1", x_words[1])
        raw_w[0, 0] = load_rows("w1_0", w1[0:K_PASS, :])
        for r in (2, 3):
            for z in range(PASSES):
                load_scale_rows(x_plane, 4 * z, x_scales[z], r)
        raw_w[1, 0] = load_rows("w2_0", w2[0:K_PASS, :])
        raw_w[0, 1] = load_rows("w1_1", w1[K_PASS:K, :])
        raw_w[1, 1] = load_rows("w2_1", w2[K_PASS:K, :])
        raw_w3 = load_rows("w3", w3)
        raw_e = []
        for tiles in E_LOADS:
            first = len(raw_e) * EDGE_TILE
            raw = load_rows("e%d" % first, eT[:, first : first + tiles * EDGE_TILE])
            raw_e.extend([raw[:, :, a * EDGE_TILE : (a + 1) * EDGE_TILE] for a in range(tiles)])
        w4_codes = load_words("w4_codes", w4_words[0])
        for r in range(4):
            load_scale_rows(w4_plane, 0, w4_scales[0], r)

        h_bank = [psum.tile([P, PACK, EDGE_TILE], F32, name="h_bank%d" % c) for c in range(EDGE_TILES)]
        out_bank = [psum.tile([P, V], F32, name="out_bank%d" % c) for c in range(EDGE_TILES)]

        def gather_words(z, picked):
            nc.vector.tensor_copy(picked[:], x_table[z][:].indirect(offsets[:]))
            return picked

        def hidden_pass(c, w_mx, codes, scales, first, last):
            for t in range(PACK):
                cols = slice(t % 2 * P, (t % 2 + 1) * P)
                nc.tensor.matmul_mx(
                    out=h_bank[c][:, t, :],
                    lhsT=w_mx[t // 2][0][:, cols].bitcast(FP8X4),
                    lhsT_scale=w_mx[t // 2][1][:, cols],
                    rhs=codes.bitcast(FP8X4),
                    rhs_scale=scales,
                    start=(first and t == 0),
                    stop=(last and t == PACK - 1),
                )

        def node_pass(side, z, picked, w_mx):
            for c in range(EDGE_TILES):
                cols = slice(side * V + c * EDGE_TILE, side * V + (c + 1) * EDGE_TILE)
                hidden_pass(c, w_mx, picked[:, cols], picked_plane[4 * z : P, cols], side == 0 and z == 0, False)

        picked_plane = keep.tile([P, S], U8, name="picked_plane", align_bytes=64)
        w_mx = {}
        picked = {}
        for z in range(PASSES):
            picked[z] = gather_words(z, keep.tile([P, S], U32, name="picked%d" % z, align_bytes=64))
        nc.vector.tensor_copy(picked_plane[:], x_plane[:].indirect(offsets[:]))
        planes = [reuse.tile([P, H // 2], U8, name="w1_0_scales%d" % a, align_bytes=64, offset=a * H // 2) for a in range(2)]
        w_mx[0, 0] = weights_mx("w1_0", raw_w[0, 0], (nc.scalar.copy, nc.scalar.copy), planes)
        shared = (nc.vector.tensor_copy, nc.scalar.copy)
        node_pass(0, 0, picked[0], w_mx[0, 0])
        for side, z in ((1, 0), (0, 1), (1, 1)):
            name = "w%d_%d" % (side + 1, z)
            w_mx[side, z] = weights_mx(name, raw_w[side, z], shared if z else (nc.scalar.copy, nc.scalar.copy))
            node_pass(side, z, picked[z], w_mx[side, z])
        w3_mx = weights_mx("w3", raw_w3, shared)

        for c in range(EDGE_TILES):
            e_mx = quantize("e%d" % c, round_edges("e%d" % c, raw_e[c], VECTOR_EDGES[c]))
            hidden_pass(c, w3_mx, e_mx[0][:], e_mx[1][:], False, True)

        def second_product(c):
            h_grouped = keep.tile([P, EDGE_TILE * PACK], BF16, name="h_grouped%d" % c, align_bytes=64)
            nc.scalar.activation(
                out=h_grouped[:].rearrange("p (v t) -> p v t", t=PACK),
                in_=h_bank[c][:].rearrange("p t v -> p v t"),
                func=GELU,
            )
            h_codes = pair.tile([P, EDGE_TILE], U32, name="h_codes", align_bytes=64)
            h_scales = pair.tile([P, EDGE_TILE], U8, name="h_scales", align_bytes=64)
            nc.vector.quantize_mx(out=h_codes[:].bitcast(FP8X4), scales=h_scales[:], in_=h_grouped[:])
            h_mx = (h_codes, h_scales)
            nc.tensor.matmul_mx(
                out=out_bank[c][:, 0:EDGE_TILE],
                lhsT=w4_codes[:].bitcast(FP8X4),
                lhsT_scale=w4_plane[:],
                rhs=h_mx[0][:].bitcast(FP8X4),
                rhs_scale=h_mx[1][:],
                start=True,
                stop=True,
            )

        def store(c):
            result = keep.tile([P, EDGE_TILE], F32, name="result%d" % c, align_bytes=256)
            nc.vector.tensor_copy(out=result[:], in_=out_bank[c][:, 0:EDGE_TILE])
            nc.sync.dma_start(out=out[:, c * EDGE_TILE : (c + 1) * EDGE_TILE], in_=result[:])

        for c in range(EDGE_TILES + 1):
            if c < EDGE_TILES:
                second_product(c)
            if c > 0:
                store(c - 1)
